import numpy as np
import ml_dtypes


def mxq(x, axis, fmt="e4m3"):
    dtype, down = {"e4m3": (ml_dtypes.float8_e4m3fn, 7), "e5m2": (ml_dtypes.float8_e5m2, 14)}[fmt]
    v = np.moveaxis(np.asarray(x, np.float32).astype(ml_dtypes.bfloat16).astype(np.float64), axis, -1)
    blocks = v.reshape(v.shape[:-1] + (-1, 32))
    amax = np.abs(blocks).max(-1, keepdims=True)
    byte = np.maximum(np.where(amax > 0, np.frexp(amax)[1] - 1 + 127, 0) - down, 1)
    scale = np.exp2(byte - 127.0)
    codes = (blocks / scale).astype(np.float32).astype(dtype).astype(np.float64)
    return np.moveaxis((codes * scale).reshape(v.shape), -1, axis)


WIDE = False


def mx_kscale(k):
    if not WIDE:
        return np.ones(k)
    levels = np.array([18, -18])
    if k % 512:
        return np.exp2(np.random.permutation(np.resize(levels, k // 32))).repeat(32)
    a = np.empty((k // 512, 16))
    for p in range(k // 512):
        a[p, :8] = np.random.permutation(np.resize(levels, 8))
        for g in range(8):
            far = levels[np.abs(levels - a[p, g]) >= 10]
            a[p, g + 8] = far[np.random.randint(len(far))]
    return np.exp2(a.ravel()).repeat(32)


def f64(x):
    return np.asarray(x).astype(np.float64)


def striped(idx):
    return np.tile(np.asarray(idx).reshape(-1, 16).T, (8, 1)).astype(np.uint16)


def unstriped(offs):
    return offs[:16].T.reshape(-1).astype(np.int64)


B, N, T, D, R = 1, 512, 2048, 512, 1024


def setup_inputs():
    n = np.random.standard_normal
    idx = np.random.permutation(T)[:B * N]
    s = mx_kscale(D)[:, None]
    z = mx_kscale(R)[:, None]
    x = n((B, D, R))
    return {
        "xT": (x * s).astype(np.float32),
        "wT": (n((D, T)) * (1.00 / np.sqrt(D)) / s).astype(np.float32),
        "y": n((B, R, N)).astype(np.float32),
        "wt": (np.random.uniform(0.5, 1.5, (B, R, 1)) * 1.0 / np.sqrt(R) * z).astype(np.float32),
        "xm": (x.transpose(0, 2, 1) / z).astype(np.float32),
        "offs": striped(idx),
    }


def reference(xT, wT, y, wt, xm, offs):
    idx = unstriped(offs)
    pick = lambda x: x[:, idx].reshape(x.shape[0], B, N).transpose(1, 0, 2)
    a = mxq(f64(xT), 1, "e4m3").transpose(0, 2, 1) @ mxq(pick(f64(wT)), 1, "e4m3")
    q = a - f64(y)
    g = f64(wt) * q * np.exp(-0.5 * q * q)
    dw = mxq(f64(xm), 1, "e4m3").transpose(0, 2, 1) @ mxq(g, 1, "e5m2")
    gw = np.zeros((D, T))
    gw[:, idx] = dw.transpose(1, 0, 2).reshape(D, B * N)
    return gw

@@ -1,0 +1,226 @@
+from contextlib import ExitStack
+
+import concourse.mybir as mybir
+
+N, T, D, R = 512, 2048, 512, 1024
+FLOPS = 2 * 2 * N * D * R
+
+F32 = mybir.dt.float32
+BF16 = mybir.dt.bfloat16
+U32 = mybir.dt.uint32
+U16 = mybir.dt.uint16
+U8 = mybir.dt.uint8
+E4M3 = mybir.dt.float8_e4m3fn_x4
+E5M2 = mybir.dt.float8_e5m2_x4
+ALU = mybir.AluOpType
+ACT = mybir.ActivationFunctionType
+
+P = 128
+PACK = 4
+K_PASS = P * PACK
+PASSES = R // K_PASS
+HALVES = 2
+NH = N // HALVES
+PAIRS = 2
+D_TILES = D // P
+WINDOWS = 3
+
+
+def tile_attend_gwel_w_kernel(tc, xT, wT, y, wt, xm, offs, out):
+    nc = tc.nc
+    with ExitStack() as ctx:
+        keep = ctx.enter_context(tc.tile_pool(name="keep", bufs=1))
+        score_psum = ctx.enter_context(tc.psum_pool(name="score_psum", bufs=4))
+        grad_psum = ctx.enter_context(tc.psum_pool(name="grad_psum", bufs=1))
+
+        def sbuf(shape, dtype, name):
+            return keep.tile(shape, dtype, name=name, align_bytes=64)
+
+        offsets = keep.tile([P, N // 16], U16, name="offsets")
+        xT_rows = xT[0].rearrange("(p j) r -> p j r", j=PACK)
+        xT_raw = [[sbuf([P, PACK, K_PASS // 2], F32, f"xT_raw{g}_{c}") for c in range(2)] for g in range(PASSES)]
+        w_planes = wT.rearrange("(p j) c -> p j c", j=PACK)
+        w_raw = [sbuf([P, T], F32, f"w_raw{j}") for j in range(PACK)]
+        y_rows = y[0].rearrange("(g p t) n -> g p t n", g=PASSES, t=PACK)
+        y_sb = [[sbuf([P, 2, N], F32, f"y{g}_{u}") for u in range(PAIRS)] for g in range(PASSES)]
+        xm_rows = xm[0].rearrange("(g p t) d -> g p t d", g=PASSES, t=PACK)
+        xm_raw = sbuf([P, PASSES, PACK, D], F32, "xm_raw")
+        wt_sb = sbuf([P, PASSES, PACK], F32, "wt_sb")
+
+        def load_xT(g, c):
+            c0 = g * K_PASS + c * (K_PASS // 2)
+            nc.sync.dma_start(out=xT_raw[g][c][:], in_=xT_rows[:, :, c0 : c0 + K_PASS // 2])
+
+        def load_y(g):
+            for u in range(PAIRS):
+                nc.sync.dma_start(out=y_sb[g][u][:], in_=y_rows[g, :, 2 * u : 2 * u + 2, :])
+
+        nc.sync.dma_start(out=w_raw[0][:], in_=w_planes[:, 0, :])
+        nc.sync.dma_start(offsets[:], offs)
+        nc.sync.dma_start(out=wt_sb[:], in_=wt[0].rearrange("(g p t) o -> p g (t o)", g=PASSES, t=PACK))
+        for j in range(1, PACK):
+            nc.sync.dma_start(out=w_raw[j][:], in_=w_planes[:, j, :])
+        load_xT(0, 0)
+        load_xT(0, 1)
+        load_xT(1, 0)
+        load_y(0)
+        load_xT(1, 1)
+        load_y(1)
+        for g in range(PASSES):
+            nc.sync.dma_start(out=xm_raw[:, g, :, :], in_=xm_rows[g])
+
+        warm = sbuf([P, 8], F32, "warm")
+        warm2 = sbuf([P, 8], F32, "warm2")
+        nc.vector.memset(warm[:], 0.0)
+        nc.scalar.activation(warm2[:], warm[:], ACT.Exp)
+
+        windows = [sbuf([P, T], F32, f"window{k}") for k in range(WINDOWS)]
+        for k in range(WINDOWS):
+            nc.vector.memset(windows[k][:], 0.0)
+
+        x_codes = [sbuf([P, PACK * P], U32, f"x_codes{g}") for g in range(PASSES)]
+        x_scales = [sbuf([P, PACK * P], U8, f"x_scales{g}") for g in range(PASSES)]
+        x_bf = [sbuf([P, PACK, P, PACK], BF16, f"x_bf{g}") for g in range(PASSES)]
+
+        def deal_xT(g):
+            for c, copy in enumerate((nc.scalar.copy, nc.vector.tensor_copy)):
+                copy(
+                    out=x_bf[g][:, :, c * (P // 2) : (c + 1) * (P // 2), :].rearrange("p t m j -> p m j t"),
+                    in_=xT_raw[g][c][:].rearrange("p j (m t) -> p m j t", t=PACK),
+                )
+
+        def quantize_xT(g):
+            nc.vector.quantize_mx(
+                out=x_codes[g][:].bitcast(E4M3),
+                scales=x_scales[g][:],
+                in_=x_bf[g][:].rearrange("p t m j -> p (t m j)"),
+            )
+
+        w_bf = sbuf([P, N, PACK], BF16, "w_bf")
+        w_codes = sbuf([P, N], U32, "w_codes")
+        w_scales = sbuf([P, N], U8, "w_scales")
+        for j in range(PACK):
+            nc.vector.tensor_copy(w_bf[:, :, j], w_raw[j][:].indirect(offsets[:]))
+        nc.vector.quantize_mx(
+            out=w_codes[:].bitcast(E4M3), scales=w_scales[:], in_=w_bf[:].rearrange("p n j -> p (n j)")
+        )
+        deal_xT(0)
+        for u in range(PAIRS):
+            nc.vector.quantize_mx(
+                out=x_codes[0][:, 2 * u * P : 2 * (u + 1) * P].bitcast(E4M3),
+                scales=x_scales[0][:, 2 * u * P : 2 * (u + 1) * P],
+                in_=x_bf[0][:, 2 * u : 2 * u + 2, :, :].rearrange("p t m j -> p (t m j)"),
+            )
+        deal_xT(1)
+        quantize_xT(1)
+
+        g_codes = [sbuf([P, N], U32, f"g_codes{g}") for g in range(PASSES)]
+        g_scales = [sbuf([P, N], U8, f"g_scales{g}") for g in range(PASSES)]
+        units = [(0, [t], slice(0, N)) for t in range(PACK)]
+        units = units + [(1, [2 * u, 2 * u + 1], slice(h * NH, (h + 1) * NH)) for h in range(HALVES) for u in range(PAIRS)]
+        g_planes0 = sbuf([P, PACK, N], BF16, "g_planes0")
+        g_planes1 = [sbuf([P, PACK, NH], BF16, f"g_planes1_{h}") for h in range(HALVES)]
+
+        def planes(g, slots):
+            return g_planes0[:, :, slots] if g == 0 else g_planes1[slots.start // NH][:]
+
+        q_sb, s_sb, e_sb = {}, {}, {}
+
+        def front(n):
+            g, places, slots = units[n]
+            width = slots.stop - slots.start
+            bank = score_psum.tile([P, len(places), width], F32, name="bank")
+            for i, t in enumerate(places):
+                nc.tensor.matmul_mx(
+                    out=bank[:, i, :],
+                    lhsT=x_codes[g][:, t * P : (t + 1) * P].bitcast(E4M3),
+                    lhsT_scale=x_scales[g][:, t * P : (t + 1) * P],
+                    rhs=w_codes[:, slots].bitcast(E4M3),
+                    rhs_scale=w_scales[:, slots],
+                    start=True,
+                    stop=True,
+                )
+            t0 = places[0]
+            q_sb[n] = sbuf([P, len(places), width], F32, f"q{n}")
+            targets = y_sb[g][t0 // 2][:, t0 % 2 : t0 % 2 + len(places), slots]
+            nc.vector.tensor_tensor(q_sb[n][:], bank[:], targets, ALU.subtract)
+            s_sb[n] = sbuf([P, len(places), width], F32, f"s{n}")
+            nc.scalar.activation(s_sb[n][:], q_sb[n][:], ACT.Square)
+
+        def middle(n):
+            e_sb[n] = sbuf(list(s_sb[n].shape), F32, f"e{n}")
+            nc.scalar.activation(e_sb[n][:], s_sb[n][:], ACT.Exp, scale=-0.5)
+
+        def back(n):
+            g, places, slots = units[n]
+            for i, t in enumerate(places):
+                nc.vector.scalar_tensor_tensor(
+                    planes(g, slots)[:, t, :],
+                    q_sb[n][:, i, :],
+                    wt_sb[:, g, t : t + 1],
+                    e_sb[n][:, i, :],
+                    ALU.mult,
+                    ALU.mult,
+                )
+
+        def weave(copy, dst, src):
+            copy(
+                out=dst.rearrange("p (c i) t -> p c t i", i=4),
+                in_=src.rearrange("p t (c i) -> p c t i", i=4),
+            )
+
+        def pack_g(g, h, copy):
+            woven = sbuf([P, NH, PACK], BF16, f"g_woven{g}{h}")
+            weave(copy, woven[:], planes(g, slice(h * NH, (h + 1) * NH)))
+            nc.vector.quantize_mx(
+                out=g_codes[g][:, h * NH : (h + 1) * NH].bitcast(E5M2),
+                scales=g_scales[g][:, h * NH : (h + 1) * NH],
+                in_=woven[:].rearrange("p n t -> p (n t)"),
+            )
+
+        for n in range(len(units) + 2):
+            if n < len(units):
+                front(n)
+            if 1 <= n <= len(units):
+                middle(n - 1)
+            if n >= 2:
+                back(n - 2)
+
+        m_codes, m_scales = {}, {}
+
+        def pack_xm(k):
+            woven = sbuf([P, PASSES, P, PACK], BF16, f"m_woven{k}")
+            for g in range(PASSES):
+                weave(nc.scalar.copy, woven[:, g, :, :], xm_raw[:, g, :, k * P : (k + 1) * P])
+            m_codes[k] = sbuf([P, PASSES * P], U32, f"m_codes{k}")
+            m_scales[k] = sbuf([P, PASSES * P], U8, f"m_scales{k}")
+            nc.vector.quantize_mx(
+                out=m_codes[k][:].bitcast(E4M3),
+                scales=m_scales[k][:],
+                in_=woven[:].rearrange("p g d t -> p (g d t)"),
+            )
+
+        def finish(k):
+            acc = grad_psum.tile([P, N], F32, name=f"acc{k}")
+            for g in range(PASSES):
+                nc.tensor.matmul_mx(
+                    out=acc[:],
+                    lhsT=m_codes[k][:, g * P : (g + 1) * P].bitcast(E4M3),
+                    lhsT_scale=m_scales[k][:, g * P : (g + 1) * P],
+                    rhs=g_codes[g][:].bitcast(E5M2),
+                    rhs_scale=g_scales[g][:],
+                    start=(g == 0),
+                    stop=(g == PASSES - 1),
+                )
+            dw = sbuf([P, N], F32, f"dw{k}")
+            nc.scalar.copy(out=dw[:], in_=acc[:])
+            nc.vector.tensor_copy(windows[k % WINDOWS][:].indirect(offsets[:]), dw[:])
+            nc.sync.dma_start(out=out[k * P : (k + 1) * P, :], in_=windows[k % WINDOWS][:])
+
+        for g in range(PASSES):
+            for h in range(HALVES):
+                pack_g(g, h, nc.vector.tensor_copy)
+        for k in range(D_TILES):
+            pack_xm(k)
+        for k in range(D_TILES):
+            finish(k)

@@ -20,187 +20,145 @@ PACK = 4
 K_PASS = P * PACK
 PASSES = R // K_PASS
 HALVES = 2
-NH = N // HALVES
-PAIRS = 2
 D_TILES = D // P
 WINDOWS = 3
+SCORE_BANKS = 4
+EXP_LAG = 2
+PRODUCT_LAG = 3
 
 
 def tile_attend_gwel_w_kernel(tc, xT, wT, y, wt, xm, offs, out):
     nc = tc.nc
     with ExitStack() as ctx:
         keep = ctx.enter_context(tc.tile_pool(name="keep", bufs=1))
-        score_psum = ctx.enter_context(tc.psum_pool(name="score_psum", bufs=4))
+        score_psum = ctx.enter_context(tc.psum_pool(name="score_psum", bufs=SCORE_BANKS))
         grad_psum = ctx.enter_context(tc.psum_pool(name="grad_psum", bufs=1))
 
         def sbuf(shape, dtype, name):
             return keep.tile(shape, dtype, name=name, align_bytes=64)
 
+        def half(h, width):
+            return slice(h * width // HALVES, (h + 1) * width // HALVES)
+
+        def quantize(codes, scales, values, fmt):
+            nc.vector.quantize_mx(out=codes.bitcast(fmt), scales=scales, in_=values)
+
+        def weave(copy, dst, src):
+            copy(out=dst.rearrange("p (c i) t -> p c t i", i=4), in_=src.rearrange("p t (c i) -> p c t i", i=4))
+
         offsets = keep.tile([P, N // 16], U16, name="offsets")
-        xT_rows = xT[0].rearrange("(p j) r -> p j r", j=PACK)
-        xT_raw = [[sbuf([P, PACK, K_PASS // 2], F32, f"xT_raw{g}_{c}") for c in range(2)] for g in range(PASSES)]
-        w_planes = wT.rearrange("(p j) c -> p j c", j=PACK)
         w_raw = [sbuf([P, T], F32, f"w_raw{j}") for j in range(PACK)]
-        y_rows = y[0].rearrange("(g p t) n -> g p t n", g=PASSES, t=PACK)
-        y_sb = [[sbuf([P, 2, N], F32, f"y{g}_{u}") for u in range(PAIRS)] for g in range(PASSES)]
-        xm_rows = xm[0].rearrange("(g p t) d -> g p t d", g=PASSES, t=PACK)
+        xT_raw = [[sbuf([P, PACK, K_PASS // HALVES], F32, f"xT_raw{g}_{h}") for h in range(HALVES)] for g in range(PASSES)]
+        tiles = [(g, t) for g in range(PASSES) for t in range(PACK)]
+        y_sb = [sbuf([P, N], F32, f"y{g}_{t}") for g, t in tiles]
         xm_raw = sbuf([P, PASSES, PACK, D], F32, "xm_raw")
         wt_sb = sbuf([P, PASSES, PACK], F32, "wt_sb")
 
-        def load_xT(g, c):
-            c0 = g * K_PASS + c * (K_PASS // 2)
-            nc.sync.dma_start(out=xT_raw[g][c][:], in_=xT_rows[:, :, c0 : c0 + K_PASS // 2])
-
-        def load_y(g):
-            for u in range(PAIRS):
-                nc.sync.dma_start(out=y_sb[g][u][:], in_=y_rows[g, :, 2 * u : 2 * u + 2, :])
+        w_planes = wT.rearrange("(p j) c -> p j c", j=PACK)
+        xT_planes = xT[0].rearrange("(p j) (g r) -> g p j r", j=PACK, g=PASSES)
+        y_rows = y[0].rearrange("(g p t) n -> g p t n", g=PASSES, t=PACK)
+        xm_rows = xm[0].rearrange("(g p t) d -> g p t d", g=PASSES, t=PACK)
 
         nc.sync.dma_start(out=w_raw[0][:], in_=w_planes[:, 0, :])
         nc.sync.dma_start(offsets[:], offs)
         nc.sync.dma_start(out=wt_sb[:], in_=wt[0].rearrange("(g p t) o -> p g (t o)", g=PASSES, t=PACK))
         for j in range(1, PACK):
             nc.sync.dma_start(out=w_raw[j][:], in_=w_planes[:, j, :])
-        load_xT(0, 0)
-        load_xT(0, 1)
-        load_xT(1, 0)
-        load_y(0)
-        load_xT(1, 1)
-        load_y(1)
+        for g in range(PASSES):
+            for h in range(HALVES):
+                nc.sync.dma_start(out=xT_raw[g][h][:], in_=xT_planes[g, :, :, half(h, K_PASS)])
+        for n, (g, t) in enumerate(tiles):
+            nc.sync.dma_start(out=y_sb[n][:], in_=y_rows[g, :, t, :])
         for g in range(PASSES):
             nc.sync.dma_start(out=xm_raw[:, g, :, :], in_=xm_rows[g])
 
-        warm = sbuf([P, 8], F32, "warm")
-        warm2 = sbuf([P, 8], F32, "warm2")
-        nc.vector.memset(warm[:], 0.0)
-        nc.scalar.activation(warm2[:], warm[:], ACT.Exp)
-
         windows = [sbuf([P, T], F32, f"window{k}") for k in range(WINDOWS)]
-        for k in range(WINDOWS):
-            nc.vector.memset(windows[k][:], 0.0)
-
-        x_codes = [sbuf([P, PACK * P], U32, f"x_codes{g}") for g in range(PASSES)]
-        x_scales = [sbuf([P, PACK * P], U8, f"x_scales{g}") for g in range(PASSES)]
-        x_bf = [sbuf([P, PACK, P, PACK], BF16, f"x_bf{g}") for g in range(PASSES)]
-
-        def deal_xT(g):
-            for c, copy in enumerate((nc.scalar.copy, nc.vector.tensor_copy)):
-                copy(
-                    out=x_bf[g][:, :, c * (P // 2) : (c + 1) * (P // 2), :].rearrange("p t m j -> p m j t"),
-                    in_=xT_raw[g][c][:].rearrange("p j (m t) -> p m j t", t=PACK),
-                )
-
-        def quantize_xT(g):
-            nc.vector.quantize_mx(
-                out=x_codes[g][:].bitcast(E4M3),
-                scales=x_scales[g][:],
-                in_=x_bf[g][:].rearrange("p t m j -> p (t m j)"),
-            )
+        for window in windows:
+            nc.vector.memset(window[:], 0.0)
 
         w_bf = sbuf([P, N, PACK], BF16, "w_bf")
         w_codes = sbuf([P, N], U32, "w_codes")
         w_scales = sbuf([P, N], U8, "w_scales")
         for j in range(PACK):
             nc.vector.tensor_copy(w_bf[:, :, j], w_raw[j][:].indirect(offsets[:]))
-        nc.vector.quantize_mx(
-            out=w_codes[:].bitcast(E4M3), scales=w_scales[:], in_=w_bf[:].rearrange("p n j -> p (n j)")
-        )
-        deal_xT(0)
-        for u in range(PAIRS):
-            nc.vector.quantize_mx(
-                out=x_codes[0][:, 2 * u * P : 2 * (u + 1) * P].bitcast(E4M3),
-                scales=x_scales[0][:, 2 * u * P : 2 * (u + 1) * P],
-                in_=x_bf[0][:, 2 * u : 2 * u + 2, :, :].rearrange("p t m j -> p (t m j)"),
-            )
-        deal_xT(1)
-        quantize_xT(1)
+        quantize(w_codes[:], w_scales[:], w_bf[:].rearrange("p n j -> p (n j)"), E4M3)
 
+        x_bf = [sbuf([P, PACK, P, PACK], BF16, f"x_bf{g}") for g in range(PASSES)]
+        x_codes = [sbuf([P, K_PASS], U32, f"x_codes{g}") for g in range(PASSES)]
+        x_scales = [sbuf([P, K_PASS], U8, f"x_scales{g}") for g in range(PASSES)]
+
+        def deal_xT(g, h, copy):
+            copy(
+                out=x_bf[g][:, :, half(h, P), :].rearrange("p t m j -> p m j t"),
+                in_=xT_raw[g][h][:].rearrange("p j (m t) -> p m j t", t=PACK),
+            )
+
+        deal_xT(0, 0, nc.scalar.copy)
+        deal_xT(0, 1, nc.vector.tensor_copy)
+        for h in range(HALVES):
+            values = x_bf[0][:, half(h, PACK), :, :].rearrange("p t m j -> p (t m j)")
+            quantize(x_codes[0][:, half(h, K_PASS)], x_scales[0][:, half(h, K_PASS)], values, E4M3)
+        deal_xT(1, 0, nc.scalar.copy)
+        deal_xT(1, 1, nc.scalar.copy)
+        quantize(x_codes[1][:], x_scales[1][:], x_bf[1][:].rearrange("p t m j -> p (t m j)"), E4M3)
+
+        q_sb = [sbuf([P, N], F32, f"q{g}_{t}") for g, t in tiles]
+        sq_sb = [sbuf([P, N], F32, f"sq{g}_{t}") for g, t in tiles]
+        e_sb = [sbuf([P, N], F32, f"e{g}_{t}") for g, t in tiles]
+        g_planes = [sbuf([P, PACK, N], BF16, f"g_planes{g}") for g in range(PASSES)]
         g_codes = [sbuf([P, N], U32, f"g_codes{g}") for g in range(PASSES)]
         g_scales = [sbuf([P, N], U8, f"g_scales{g}") for g in range(PASSES)]
-        units = [(0, [t], slice(0, N)) for t in range(PACK)]
-        units = units + [(1, [2 * u, 2 * u + 1], slice(h * NH, (h + 1) * NH)) for h in range(HALVES) for u in range(PAIRS)]
-        g_planes0 = sbuf([P, PACK, N], BF16, "g_planes0")
-        g_planes1 = [sbuf([P, PACK, NH], BF16, f"g_planes1_{h}") for h in range(HALVES)]
 
-        def planes(g, slots):
-            return g_planes0[:, :, slots] if g == 0 else g_planes1[slots.start // NH][:]
+        def residual(n):
+            g, t = tiles[n]
+            bank = score_psum.tile([P, N], F32, name="bank")
+            nc.tensor.matmul_mx(
+                out=bank[:],
+                lhsT=x_codes[g][:, t * P : (t + 1) * P].bitcast(E4M3),
+                lhsT_scale=x_scales[g][:, t * P : (t + 1) * P],
+                rhs=w_codes[:].bitcast(E4M3),
+                rhs_scale=w_scales[:],
+                start=True,
+                stop=True,
+            )
+            nc.vector.tensor_tensor(q_sb[n][:], bank[:], y_sb[n][:], ALU.subtract)
+            nc.scalar.activation(sq_sb[n][:], q_sb[n][:], ACT.Square)
 
-        q_sb, s_sb, e_sb = {}, {}, {}
-
-        def front(n):
-            g, places, slots = units[n]
-            width = slots.stop - slots.start
-            bank = score_psum.tile([P, len(places), width], F32, name="bank")
-            for i, t in enumerate(places):
-                nc.tensor.matmul_mx(
-                    out=bank[:, i, :],
-                    lhsT=x_codes[g][:, t * P : (t + 1) * P].bitcast(E4M3),
-                    lhsT_scale=x_scales[g][:, t * P : (t + 1) * P],
-                    rhs=w_codes[:, slots].bitcast(E4M3),
-                    rhs_scale=w_scales[:, slots],
-                    start=True,
-                    stop=True,
-                )
-            t0 = places[0]
-            q_sb[n] = sbuf([P, len(places), width], F32, f"q{n}")
-            targets = y_sb[g][t0 // 2][:, t0 % 2 : t0 % 2 + len(places), slots]
-            nc.vector.tensor_tensor(q_sb[n][:], bank[:], targets, ALU.subtract)
-            s_sb[n] = sbuf([P, len(places), width], F32, f"s{n}")
-            nc.scalar.activation(s_sb[n][:], q_sb[n][:], ACT.Square)
-
-        def middle(n):
-            e_sb[n] = sbuf(list(s_sb[n].shape), F32, f"e{n}")
-            nc.scalar.activation(e_sb[n][:], s_sb[n][:], ACT.Exp, scale=-0.5)
-
-        def back(n):
-            g, places, slots = units[n]
-            for i, t in enumerate(places):
-                nc.vector.scalar_tensor_tensor(
-                    planes(g, slots)[:, t, :],
-                    q_sb[n][:, i, :],
-                    wt_sb[:, g, t : t + 1],
-                    e_sb[n][:, i, :],
-                    ALU.mult,
-                    ALU.mult,
-                )
-
-        def weave(copy, dst, src):
-            copy(
-                out=dst.rearrange("p (c i) t -> p c t i", i=4),
-                in_=src.rearrange("p t (c i) -> p c t i", i=4),
+        def gradient(n):
+            g, t = tiles[n]
+            nc.vector.scalar_tensor_tensor(
+                g_planes[g][:, t, :], q_sb[n][:], wt_sb[:, g, t : t + 1], e_sb[n][:], ALU.mult, ALU.mult
             )
 
-        def pack_g(g, h, copy):
-            woven = sbuf([P, NH, PACK], BF16, f"g_woven{g}{h}")
-            weave(copy, woven[:], planes(g, slice(h * NH, (h + 1) * NH)))
-            nc.vector.quantize_mx(
-                out=g_codes[g][:, h * NH : (h + 1) * NH].bitcast(E5M2),
-                scales=g_scales[g][:, h * NH : (h + 1) * NH],
-                in_=woven[:].rearrange("p n t -> p (n t)"),
-            )
+        def pack_g(g):
+            for h in range(HALVES):
+                woven = sbuf([P, N // HALVES, PACK], BF16, f"g_woven{g}_{h}")
+                weave(nc.vector.tensor_copy, woven[:], g_planes[g][:, :, half(h, N)])
+                values = woven[:].rearrange("p n t -> p (n t)")
+                quantize(g_codes[g][:, half(h, N)], g_scales[g][:, half(h, N)], values, E5M2)
 
-        for n in range(len(units) + 2):
-            if n < len(units):
-                front(n)
-            if 1 <= n <= len(units):
-                middle(n - 1)
-            if n >= 2:
-                back(n - 2)
-
-        m_codes, m_scales = {}, {}
+        m_codes = [sbuf([P, PASSES * P], U32, f"m_codes{k}") for k in range(D_TILES)]
+        m_scales = [sbuf([P, PASSES * P], U8, f"m_scales{k}") for k in range(D_TILES)]
 
         def pack_xm(k):
             woven = sbuf([P, PASSES, P, PACK], BF16, f"m_woven{k}")
             for g in range(PASSES):
                 weave(nc.scalar.copy, woven[:, g, :, :], xm_raw[:, g, :, k * P : (k + 1) * P])
-            m_codes[k] = sbuf([P, PASSES * P], U32, f"m_codes{k}")
-            m_scales[k] = sbuf([P, PASSES * P], U8, f"m_scales{k}")
-            nc.vector.quantize_mx(
-                out=m_codes[k][:].bitcast(E4M3),
-                scales=m_scales[k][:],
-                in_=woven[:].rearrange("p g d t -> p (g d t)"),
-            )
+            quantize(m_codes[k][:], m_scales[k][:], woven[:].rearrange("p g d t -> p (g d t)"), E4M3)
 
-        def finish(k):
+        for n in range(len(tiles) + PRODUCT_LAG):
+            if n < len(tiles):
+                residual(n)
+            if EXP_LAG <= n < len(tiles) + EXP_LAG:
+                nc.scalar.activation(e_sb[n - EXP_LAG][:], sq_sb[n - EXP_LAG][:], ACT.Exp, scale=-0.5)
+            if n >= PRODUCT_LAG:
+                gradient(n - PRODUCT_LAG)
+            if n - PRODUCT_LAG == PACK - 1:
+                pack_g(0)
+        pack_xm(0)
+        pack_g(1)
+
+        def finish(k, copy):
             acc = grad_psum.tile([P, N], F32, name=f"acc{k}")
             for g in range(PASSES):
                 nc.tensor.matmul_mx(
@@ -213,14 +171,13 @@ def tile_attend_gwel_w_kernel(tc, xT, wT, y, wt, xm, offs, out):
                     stop=(g == PASSES - 1),
                 )
             dw = sbuf([P, N], F32, f"dw{k}")
-            nc.scalar.copy(out=dw[:], in_=acc[:])
-            nc.vector.tensor_copy(windows[k % WINDOWS][:].indirect(offsets[:]), dw[:])
-            nc.sync.dma_start(out=out[k * P : (k + 1) * P, :], in_=windows[k % WINDOWS][:])
+            copy(out=dw[:], in_=acc[:])
+            window = windows[k % WINDOWS]
+            nc.vector.tensor_copy(window[:].indirect(offsets[:]), dw[:])
+            nc.sync.dma_start(out=out[k * P : (k + 1) * P, :], in_=window[:])
 
-        for g in range(PASSES):
-            for h in range(HALVES):
-                pack_g(g, h, nc.vector.tensor_copy)
-        for k in range(D_TILES):
+        finish(0, nc.vector.tensor_copy)
+        for k in range(1, D_TILES):
             pack_xm(k)
-        for k in range(D_TILES):
-            finish(k)
+        for k in range(1, D_TILES):
+            finish(k, nc.scalar.copy)

@@ -48,7 +48,7 @@ def tile_attend_gwel_w_kernel(tc, xT, wT, y, wt, xm, offs, out):
 
         offsets = keep.tile([P, N // 16], U16, name="offsets")
         w_raw = [sbuf([P, T], F32, f"w_raw{j}") for j in range(PACK)]
-        xT_raw = [[sbuf([P, PACK, K_PASS // HALVES], F32, f"xT_raw{g}_{h}") for h in range(HALVES)] for g in range(PASSES)]
+        xT_raw = [sbuf([P, PACK, K_PASS], F32, f"xT_raw{g}") for g in range(PASSES)]
         tiles = [(g, t) for g in range(PASSES) for t in range(PACK)]
         y_sb = [sbuf([P, N], F32, f"y{g}_{t}") for g, t in tiles]
         xm_raw = sbuf([P, PASSES, PACK, D], F32, "xm_raw")
@@ -61,12 +61,11 @@ def tile_attend_gwel_w_kernel(tc, xT, wT, y, wt, xm, offs, out):
 
         nc.sync.dma_start(out=w_raw[0][:], in_=w_planes[:, 0, :])
         nc.sync.dma_start(offsets[:], offs)
-        nc.sync.dma_start(out=wt_sb[:], in_=wt[0].rearrange("(g p t) o -> p g (t o)", g=PASSES, t=PACK))
+        nc.scalar.dma_start(out=wt_sb[:], in_=wt[0].rearrange("(g p t) o -> p g (t o)", g=PASSES, t=PACK))
         for j in range(1, PACK):
             nc.sync.dma_start(out=w_raw[j][:], in_=w_planes[:, j, :])
         for g in range(PASSES):
-            for h in range(HALVES):
-                nc.sync.dma_start(out=xT_raw[g][h][:], in_=xT_planes[g, :, :, half(h, K_PASS)])
+            nc.sync.dma_start(out=xT_raw[g][:], in_=xT_planes[g])
         for n, (g, t) in enumerate(tiles):
             nc.sync.dma_start(out=y_sb[n][:], in_=y_rows[g, :, t, :])
         for g in range(PASSES):
@@ -83,24 +82,20 @@ def tile_attend_gwel_w_kernel(tc, xT, wT, y, wt, xm, offs, out):
             nc.vector.tensor_copy(w_bf[:, :, j], w_raw[j][:].indirect(offsets[:]))
         quantize(w_codes[:], w_scales[:], w_bf[:].rearrange("p n j -> p (n j)"), E4M3)
 
-        x_bf = [sbuf([P, PACK, P, PACK], BF16, f"x_bf{g}") for g in range(PASSES)]
         x_codes = [sbuf([P, K_PASS], U32, f"x_codes{g}") for g in range(PASSES)]
         x_scales = [sbuf([P, K_PASS], U8, f"x_scales{g}") for g in range(PASSES)]
-
-        def deal_xT(g, h, copy):
-            copy(
-                out=x_bf[g][:, :, half(h, P), :].rearrange("p t m j -> p m j t"),
-                in_=xT_raw[g][h][:].rearrange("p j (m t) -> p m j t", t=PACK),
-            )
-
-        deal_xT(0, 0, nc.scalar.copy)
-        deal_xT(0, 1, nc.vector.tensor_copy)
-        for h in range(HALVES):
-            values = x_bf[0][:, half(h, PACK), :, :].rearrange("p t m j -> p (t m j)")
-            quantize(x_codes[0][:, half(h, K_PASS)], x_scales[0][:, half(h, K_PASS)], values, E4M3)
-        deal_xT(1, 0, nc.scalar.copy)
-        deal_xT(1, 1, nc.scalar.copy)
-        quantize(x_codes[1][:], x_scales[1][:], x_bf[1][:].rearrange("p t m j -> p (t m j)"), E4M3)
+        for g in range(PASSES):
+            dealt = sbuf([P, PACK, P, PACK], BF16, f"x_dealt{g}")
+            for h, copy in enumerate((nc.vector.tensor_copy, nc.scalar.copy)):
+                copy(
+                    out=dealt[:, half(h, PACK), :, :].rearrange("p t m j -> p m j t"),
+                    in_=xT_raw[g][:].rearrange("p j (m t) -> p m j t", t=PACK)[:, :, :, half(h, PACK)],
+                )
+                if g == 0:
+                    values = dealt[:, half(h, PACK), :, :].rearrange("p t m j -> p (t m j)")
+                    quantize(x_codes[g][:, half(h, K_PASS)], x_scales[g][:, half(h, K_PASS)], values, E4M3)
+            if g > 0:
+                quantize(x_codes[g][:], x_scales[g][:], dealt[:].rearrange("p t m j -> p (t m j)"), E4M3)
 
         q_sb = [sbuf([P, N], F32, f"q{g}_{t}") for g, t in tiles]
         sq_sb = [sbuf([P, N], F32, f"sq{g}_{t}") for g, t in tiles]

from contextlib import ExitStack

import concourse.mybir as mybir

N, T, D, R = 512, 2048, 512, 1024
FLOPS = 2 * 2 * N * D * R

F32 = mybir.dt.float32
BF16 = mybir.dt.bfloat16
U32 = mybir.dt.uint32
U16 = mybir.dt.uint16
U8 = mybir.dt.uint8
E4M3 = mybir.dt.float8_e4m3fn_x4
E5M2 = mybir.dt.float8_e5m2_x4
ALU = mybir.AluOpType
ACT = mybir.ActivationFunctionType

P = 128
PACK = 4
K_PASS = P * PACK
PASSES = R // K_PASS
HALVES = 2
D_TILES = D // P
WINDOWS = 3
SCORE_BANKS = 4
EXP_LAG = 2
PRODUCT_LAG = 3


def tile_attend_gwel_w_kernel(tc, xT, wT, y, wt, xm, offs, out):
    nc = tc.nc
    with ExitStack() as ctx:
        keep = ctx.enter_context(tc.tile_pool(name="keep", bufs=1))
        score_psum = ctx.enter_context(tc.psum_pool(name="score_psum", bufs=SCORE_BANKS))
        grad_psum = ctx.enter_context(tc.psum_pool(name="grad_psum", bufs=1))

        def sbuf(shape, dtype, name):
            return keep.tile(shape, dtype, name=name, align_bytes=64)

        def half(h, width):
            return slice(h * width // HALVES, (h + 1) * width // HALVES)

        def quantize(codes, scales, values, fmt):
            nc.vector.quantize_mx(out=codes.bitcast(fmt), scales=scales, in_=values)

        def weave(copy, dst, src):
            copy(out=dst.rearrange("p (c i) t -> p c t i", i=4), in_=src.rearrange("p t (c i) -> p c t i", i=4))

        offsets = keep.tile([P, N // 16], U16, name="offsets")
        w_raw = [sbuf([P, T], F32, f"w_raw{j}") for j in range(PACK)]
        xT_raw = [sbuf([P, PACK, K_PASS], F32, f"xT_raw{g}") for g in range(PASSES)]
        tiles = [(g, t) for g in range(PASSES) for t in range(PACK)]
        y_sb = [sbuf([P, N], F32, f"y{g}_{t}") for g, t in tiles]
        xm_raw = sbuf([P, PASSES, PACK, D], F32, "xm_raw")
        wt_sb = sbuf([P, PASSES, PACK], F32, "wt_sb")

        w_planes = wT.rearrange("(p j) c -> p j c", j=PACK)
        xT_planes = xT[0].rearrange("(p j) (g r) -> g p j r", j=PACK, g=PASSES)
        y_rows = y[0].rearrange("(g p t) n -> g p t n", g=PASSES, t=PACK)
        xm_rows = xm[0].rearrange("(g p t) d -> g p t d", g=PASSES, t=PACK)

        nc.sync.dma_start(out=w_raw[0][:], in_=w_planes[:, 0, :])
        nc.sync.dma_start(offsets[:], offs)
        nc.scalar.dma_start(out=wt_sb[:], in_=wt[0].rearrange("(g p t) o -> p g (t o)", g=PASSES, t=PACK))
        for j in range(1, PACK):
            nc.sync.dma_start(out=w_raw[j][:], in_=w_planes[:, j, :])
        for g in range(PASSES):
            nc.sync.dma_start(out=xT_raw[g][:], in_=xT_planes[g])
        for n, (g, t) in enumerate(tiles):
            nc.sync.dma_start(out=y_sb[n][:], in_=y_rows[g, :, t, :])
        for g in range(PASSES):
            nc.sync.dma_start(out=xm_raw[:, g, :, :], in_=xm_rows[g])

        windows = [sbuf([P, T], F32, f"window{k}") for k in range(WINDOWS)]
        for window in windows:
            nc.vector.memset(window[:], 0.0)

        w_bf = sbuf([P, N, PACK], BF16, "w_bf")
        w_codes = sbuf([P, N], U32, "w_codes")
        w_scales = sbuf([P, N], U8, "w_scales")
        for j in range(PACK):
            nc.vector.tensor_copy(w_bf[:, :, j], w_raw[j][:].indirect(offsets[:]))
        quantize(w_codes[:], w_scales[:], w_bf[:].rearrange("p n j -> p (n j)"), E4M3)

        x_codes = [sbuf([P, K_PASS], U32, f"x_codes{g}") for g in range(PASSES)]
        x_scales = [sbuf([P, K_PASS], U8, f"x_scales{g}") for g in range(PASSES)]
        for g in range(PASSES):
            dealt = sbuf([P, PACK, P, PACK], BF16, f"x_dealt{g}")
            for h, copy in enumerate((nc.vector.tensor_copy, nc.scalar.copy)):
                copy(
                    out=dealt[:, half(h, PACK), :, :].rearrange("p t m j -> p m j t"),
                    in_=xT_raw[g][:].rearrange("p j (m t) -> p m j t", t=PACK)[:, :, :, half(h, PACK)],
                )
                if g == 0:
                    values = dealt[:, half(h, PACK), :, :].rearrange("p t m j -> p (t m j)")
                    quantize(x_codes[g][:, half(h, K_PASS)], x_scales[g][:, half(h, K_PASS)], values, E4M3)
            if g > 0:
                quantize(x_codes[g][:], x_scales[g][:], dealt[:].rearrange("p t m j -> p (t m j)"), E4M3)

        q_sb = [sbuf([P, N], F32, f"q{g}_{t}") for g, t in tiles]
        sq_sb = [sbuf([P, N], F32, f"sq{g}_{t}") for g, t in tiles]
        e_sb = [sbuf([P, N], F32, f"e{g}_{t}") for g, t in tiles]
        g_planes = [sbuf([P, PACK, N], BF16, f"g_planes{g}") for g in range(PASSES)]
        g_codes = [sbuf([P, N], U32, f"g_codes{g}") for g in range(PASSES)]
        g_scales = [sbuf([P, N], U8, f"g_scales{g}") for g in range(PASSES)]

        def residual(n):
            g, t = tiles[n]
            bank = score_psum.tile([P, N], F32, name="bank")
            nc.tensor.matmul_mx(
                out=bank[:],
                lhsT=x_codes[g][:, t * P : (t + 1) * P].bitcast(E4M3),
                lhsT_scale=x_scales[g][:, t * P : (t + 1) * P],
                rhs=w_codes[:].bitcast(E4M3),
                rhs_scale=w_scales[:],
                start=True,
                stop=True,
            )
            nc.vector.tensor_tensor(q_sb[n][:], bank[:], y_sb[n][:], ALU.subtract)
            nc.scalar.activation(sq_sb[n][:], q_sb[n][:], ACT.Square)

        def gradient(n):
            g, t = tiles[n]
            nc.vector.scalar_tensor_tensor(
                g_planes[g][:, t, :], q_sb[n][:], wt_sb[:, g, t : t + 1], e_sb[n][:], ALU.mult, ALU.mult
            )

        def pack_g(g):
            for h in range(HALVES):
                woven = sbuf([P, N // HALVES, PACK], BF16, f"g_woven{g}_{h}")
                weave(nc.vector.tensor_copy, woven[:], g_planes[g][:, :, half(h, N)])
                values = woven[:].rearrange("p n t -> p (n t)")
                quantize(g_codes[g][:, half(h, N)], g_scales[g][:, half(h, N)], values, E5M2)

        m_codes = [sbuf([P, PASSES * P], U32, f"m_codes{k}") for k in range(D_TILES)]
        m_scales = [sbuf([P, PASSES * P], U8, f"m_scales{k}") for k in range(D_TILES)]

        def pack_xm(k):
            woven = sbuf([P, PASSES, P, PACK], BF16, f"m_woven{k}")
            for g in range(PASSES):
                weave(nc.scalar.copy, woven[:, g, :, :], xm_raw[:, g, :, k * P : (k + 1) * P])
            quantize(m_codes[k][:], m_scales[k][:], woven[:].rearrange("p g d t -> p (g d t)"), E4M3)

        for n in range(len(tiles) + PRODUCT_LAG):
            if n < len(tiles):
                residual(n)
            if EXP_LAG <= n < len(tiles) + EXP_LAG:
                nc.scalar.activation(e_sb[n - EXP_LAG][:], sq_sb[n - EXP_LAG][:], ACT.Exp, scale=-0.5)
            if n >= PRODUCT_LAG:
                gradient(n - PRODUCT_LAG)
            if n - PRODUCT_LAG == PACK - 1:
                pack_g(0)
        pack_xm(0)
        pack_g(1)

        def finish(k, copy):
            acc = grad_psum.tile([P, N], F32, name=f"acc{k}")
            for g in range(PASSES):
                nc.tensor.matmul_mx(
                    out=acc[:],
                    lhsT=m_codes[k][:, g * P : (g + 1) * P].bitcast(E4M3),
                    lhsT_scale=m_scales[k][:, g * P : (g + 1) * P],
                    rhs=g_codes[g][:].bitcast(E5M2),
                    rhs_scale=g_scales[g][:],
                    start=(g == 0),
                    stop=(g == PASSES - 1),
                )
            dw = sbuf([P, N], F32, f"dw{k}")
            copy(out=dw[:], in_=acc[:])
            window = windows[k % WINDOWS]
            nc.vector.tensor_copy(window[:].indirect(offsets[:]), dw[:])
            nc.sync.dma_start(out=out[k * P : (k + 1) * P, :], in_=window[:])

        finish(0, nc.vector.tensor_copy)
        for k in range(1, D_TILES):
            pack_xm(k)
        for k in range(1, D_TILES):
            finish(k, nc.scalar.copy)
